import numpy as np
import ml_dtypes


def mxq(x, axis, fmt="e4m3"):
    dtype, down = {"e4m3": (ml_dtypes.float8_e4m3fn, 7), "e5m2": (ml_dtypes.float8_e5m2, 14)}[fmt]
    v = np.moveaxis(np.asarray(x, np.float32).astype(ml_dtypes.bfloat16).astype(np.float64), axis, -1)
    blocks = v.reshape(v.shape[:-1] + (-1, 32))
    amax = np.abs(blocks).max(-1, keepdims=True)
    byte = np.maximum(np.where(amax > 0, np.frexp(amax)[1] - 1 + 127, 0) - down, 1)
    scale = np.exp2(byte - 127.0)
    codes = (blocks / scale).astype(np.float32).astype(dtype).astype(np.float64)
    return np.moveaxis((codes * scale).reshape(v.shape), -1, axis)


WIDE = False


def mx_kscale(k):
    if not WIDE:
        return np.ones(k)
    levels = np.array([10, -10, 5, -5, 0])
    if k % 512:
        return np.exp2(np.random.permutation(np.resize(levels, k // 32))).repeat(32)
    a = np.empty((k // 512, 16))
    for p in range(k // 512):
        a[p, :8] = np.random.permutation(np.resize(levels, 8))
        for g in range(8):
            far = levels[np.abs(levels - a[p, g]) >= 10]
            a[p, g + 8] = far[np.random.randint(len(far))]
    return np.exp2(a.ravel()).repeat(32)


BF16 = ml_dtypes.bfloat16


def bf(x):
    return np.asarray(x, np.float32).astype(BF16)


def f64(x):
    return np.asarray(x).astype(np.float64)


E2M1 = np.array([0.0, 0.5, 1.0, 1.5, 2.0, 3.0, 4.0, 6.0, -0.0, -0.5, -1.0, -1.5, -2.0, -3.0, -4.0, -6.0])


def pack_weight(w, fmt):
    k, n = w.shape
    w = f64(bf(w)).reshape(k // 32, 32, n)
    amax = np.abs(w).max(1)
    if fmt == "e4m3":
        byte = np.frexp(amax)[1] - 1 + 127 - 7
    else:
        mant, ex = np.frexp(amax / 6.0)
        byte = np.where(mant > 0.5, ex, ex - 1) + 127
    byte = np.clip(np.where(amax > 0, byte, 1), 1, 254)
    scaled = (w * np.exp2(127.0 - byte)[:, None, :]).reshape(k, n).astype(np.float32)
    by_word = np.ascontiguousarray(scaled.reshape(k // 512, 128, 4, n).transpose(0, 1, 3, 2))
    if fmt == "e4m3":
        words = by_word.astype(ml_dtypes.float8_e4m3fn).view(np.uint8)
    else:
        c = by_word.astype(ml_dtypes.float4_e2m1fn).view(np.uint8) & 0xF
        words = c[..., 0::2] | (c[..., 1::2] << 4)
    return np.ascontiguousarray(words), np.ascontiguousarray(byte.astype(np.uint8).reshape(k // 512, 16, n))


def unpack_weight(words, scales, fmt):
    g, p, n, _ = words.shape
    if fmt == "e4m3":
        vals = np.ascontiguousarray(words).view(ml_dtypes.float8_e4m3fn).astype(np.float64)
    else:
        nib = np.empty((g, p, n, 4), np.uint8)
        nib[..., 0::2] = words & 0xF
        nib[..., 1::2] = words >> 4
        vals = E2M1[nib]
    vals = vals * np.repeat(np.exp2(scales.astype(np.float64) - 127.0), 8, axis=1)[..., None]
    return vals.transpose(0, 1, 3, 2).reshape(g * 512, n)
def pack4(w):
    words, scales = pack_weight(w, "e2m1")
    return words.reshape(words.shape[0], 128, -1), scales


def unpack4(words, scales):
    return unpack_weight(words.reshape(words.shape[0], 128, -1, 2), scales, "e2m1")


M, KA, KB, N = 1024, 1024, 512, 1024


def setup_inputs():
    sa, sb, t = mx_kscale(KA), mx_kscale(KB), mx_kscale(N)
    cols = np.concatenate([t, 0.5 * np.ones(N)])
    bcols = np.concatenate([t, np.ones(N)])
    xa_words, xa_scales = pack4(np.random.standard_normal((KA, M)) * sa[:, None])
    xb_words, xb_scales = pack4(np.random.standard_normal((KB, M)) * sb[:, None])
    wa_words, wa_scales = pack4(np.random.standard_normal((KA, 2 * N)) / np.sqrt(KA) / sa[:, None] * cols)
    wb_words, wb_scales = pack4(np.random.standard_normal((KB, 2 * N)) / np.sqrt(KB) / sb[:, None] * cols)
    da_words, da_scales = pack4(np.random.standard_normal((N, KA)) / np.sqrt(N) / t[:, None])
    db_words, db_scales = pack4(np.random.standard_normal((N, KB)) / np.sqrt(N) / t[:, None])
    return {"xa_words": xa_words, "xa_scales": xa_scales,
            "xb_words": xb_words, "xb_scales": xb_scales,
            "wa_words": wa_words, "wa_scales": wa_scales,
            "wb_words": wb_words, "wb_scales": wb_scales,
            "ba": bf(0.4 * np.random.standard_normal(2 * N) * bcols),
            "bb": bf(0.4 * np.random.standard_normal(2 * N) * bcols),
            "prior_mean": bf(0.5 * np.random.standard_normal(N) * t),
            "prior_logprec": bf(0.4 * np.random.standard_normal(N)),
            "eps": bf(np.random.standard_normal((M, N)) * t),
            "da_words": da_words, "da_scales": da_scales,
            "db_words": db_words, "db_scales": db_scales,
            "ca": bf(0.3 * np.random.standard_normal(KA)),
            "cb": bf(0.3 * np.random.standard_normal(KB))}


def reference(xa_words, xa_scales, xb_words, xb_scales, wa_words, wa_scales, wb_words, wb_scales,
              ba, bb, prior_mean, prior_logprec, eps, da_words, da_scales, db_words, db_scales, ca, cb):
    ha = (unpack4(xa_words, xa_scales).T @ unpack4(wa_words, wa_scales)) + f64(ba)
    hb = (unpack4(xb_words, xb_scales).T @ unpack4(wb_words, wb_scales)) + f64(bb)
    ta = np.exp(ha[:, N:])
    tb = np.exp(hb[:, N:])
    t0 = np.exp(f64(prior_logprec))
    lam = t0 + ta + tb
    mean = (t0 * f64(prior_mean) + ta * ha[:, :N] + tb * hb[:, :N]) / lam
    z = mean + f64(eps) / np.sqrt(lam)
    zq = mxq(z, 1, "e4m3")
    ya = (zq @ unpack4(da_words, da_scales)) + f64(ca)
    yb = (zq @ unpack4(db_words, db_scales)) + f64(cb)
    return ya, yb

@@ -1,0 +1,401 @@
+from contextlib import ExitStack
+
+import concourse.mybir as mybir
+from concourse.masks import make_identity
+
+F32 = mybir.dt.float32
+BF16 = mybir.dt.bfloat16
+U8 = mybir.dt.uint8
+U32 = mybir.dt.uint32
+I32 = mybir.dt.int32
+FP4X4 = mybir.dt.float4_e2m1fn_x4
+FP8X4 = mybir.dt.float8_e4m3fn_x4
+ACT = mybir.ActivationFunctionType
+ALU = mybir.AluOpType
+
+P = 128
+M, KA, KB, N = 1024, 1024, 512, 1024
+FLOPS = 2 * M * (2 * N * (KA + KB) + N * (KA + KB))
+
+HALF = 512
+GA = 2
+KG = 3
+T = 4
+NT = N // P
+E = 2
+
+
+def tile_product_of_experts_fusion_f2_kernel(
+    tc, xa_words, xa_scales, xb_words, xb_scales, wa_words, wa_scales, wb_words, wb_scales,
+    ba, bb, prior_mean, prior_logprec, eps, da_words, da_scales, db_words, db_scales, ca, cb, out_a, out_b,
+):
+    nc = tc.nc
+    with ExitStack() as ctx:
+        keep = ctx.enter_context(tc.tile_pool(name="keep", bufs=1))
+        work = ctx.enter_context(tc.tile_pool(name="work", bufs=4))
+        twice = ctx.enter_context(tc.tile_pool(name="twice", bufs=2))
+        outs = ctx.enter_context(tc.tile_pool(name="outs", bufs=3))
+        psum = ctx.enter_context(tc.psum_pool(name="psum", bufs=1))
+        ctx.enter_context(tc.manual_schedule())
+
+        def bank(i, dt=F32):
+            return psum.tile([P, 2048 // (4 if dt == F32 else 2)], dt, tag="b%d" % i, name="b%d" % i)
+
+        xw = keep.tile([P, KG, 2 * M], U8, align_bytes=64, name="xw")
+        xs = keep.tile([P, KG, M], U8, align_bytes=64, name="xs")
+        ww = keep.tile([P, KG, 4 * N], U8, align_bytes=64, name="ww")
+        ws = keep.tile([P, KG, 2 * N], U8, align_bytes=64, name="ws")
+        dw = keep.tile([P, E, 3072], U8, align_bytes=64, name="dw")
+        dsc = keep.tile([P, E, 1536], U8, align_bytes=64, name="dsc")
+        eps_sb = keep.tile([P, 8, N], BF16, align_bytes=64, name="eps_sb")
+        lam = keep.tile([P, 2, NT, HALF], F32, align_bytes=64, name="lam")
+        num = keep.tile([P, 2, NT, HALF], F32, align_bytes=64, name="num")
+        zq = keep.tile([P, E, M], U32, align_bytes=64, name="zq")
+        zs = keep.tile([P, E, M], U8, align_bytes=64, name="zs")
+        ident = keep.tile([P, P], F32, align_bytes=64, name="ident")
+        identb = keep.tile([P, P], BF16, align_bytes=64, name="identb")
+        warm = keep.tile([P, 1], F32, name="warm")
+        warm2 = keep.tile([P, 1], F32, name="warm2")
+        rows1 = keep.tile([P, P], BF16, name="rows1")
+        rows2 = keep.tile([P, P], BF16, name="rows2")
+        v1 = keep.tile([P, 32], F32, name="v1")
+        v2 = keep.tile([P, 28], F32, name="v2")
+        t0 = keep.tile([P, NT], F32, name="t0")
+        c0 = keep.tile([P, NT], F32, name="c0")
+        cbb = keep.tile([P, KB], BF16, name="cbb")
+        cab2 = keep.tile([P, HALF], BF16, name="cab2")
+
+        nc.vector.memset(warm[:], 0.0)
+        for k in (slice(0, GA), slice(GA, KG)):
+            nc.gpsimd.memset(xs[:, k, :].rearrange("p a n -> p (a n)").bitcast(I32), 0)
+            nc.vector.memset(ws[:, k, :].rearrange("p a n -> p (a n)").bitcast(I32), 0)
+        nc.gpsimd.memset(rows1[:], 0.0)
+        nc.scalar.activation(out=warm2[:], in_=warm[:], func=ACT.Exp)
+
+        def load_scales(engs, plane, groups, cols, src):
+            for r in range(4):
+                engs[r].dma_start(
+                    out=plane[r:P:32, groups, cols].bitcast(I32),
+                    in_=src[:, r:16:4, :].bitcast(I32).rearrange("g q n -> q g n"),
+                )
+
+        def load_words(dst, src):
+            nc.sync.dma_start(out=dst.bitcast(I32), in_=src.bitcast(I32).rearrange("g p n -> p g n"))
+
+        A = slice(0, GA)
+        B = slice(GA, KG)
+
+        def wcols(c, g):
+            return slice((c * N + g * 512) * 2, (c * N + (g + 1) * 512) * 2)
+
+        def xcols(h):
+            return slice(h * 2 * HALF, (h + 1) * 2 * HALF)
+
+        load_words(ww[:, A, wcols(1, 0)], wa_words[:, :, wcols(1, 0)])
+        load_words(xw[:, A, xcols(0)], xa_words[:, :, xcols(0)])
+        load_scales([nc.scalar] * 4, xs, A, slice(0, M), xa_scales)
+        load_scales([nc.scalar, nc.scalar, nc.gpsimd, nc.gpsimd], ws, A, slice(0, 2 * N), wa_scales)
+        load_words(ww[:, B, wcols(1, 0)], wb_words[:, :, wcols(1, 0)])
+        load_words(xw[:, B, xcols(0)], xb_words[:, :, xcols(0)])
+        load_scales([nc.scalar] * 4, xs, B, slice(0, M), xb_scales)
+        load_scales([nc.scalar] * 4, ws, B, slice(0, 2 * N), wb_scales)
+        nc.gpsimd.dma_start(out=rows1[0:16, :], in_=ba.rearrange("(c p) -> c p", p=P))
+        nc.gpsimd.dma_start(out=rows1[16:32, :], in_=bb.rearrange("(c p) -> c p", p=P))
+        make_identity(nc, ident[:])
+        nc.gpsimd.memset(dsc[:].rearrange("p a n -> p (a n)").bitcast(I32), 0)
+        nc.gpsimd.memset(rows2[:], 0.0)
+        nc.gpsimd.dma_start(out=rows2[0:8, :], in_=prior_logprec.rearrange("(c p) -> c p", p=P))
+        nc.gpsimd.dma_start(out=rows2[8:16, :], in_=prior_mean.rearrange("(c p) -> c p", p=P))
+        nc.gpsimd.dma_start(out=rows2[16:24, :], in_=ca.rearrange("(c p) -> c p", p=P))
+        nc.gpsimd.dma_start(out=rows2[24:28, :], in_=cb.rearrange("(c p) -> c p", p=P))
+        for c, g in ((0, 0), (1, 1), (0, 1)):
+            load_words(ww[:, A, wcols(c, g)], wa_words[:, :, wcols(c, g)])
+            load_words(ww[:, B, wcols(c, g)], wb_words[:, :, wcols(c, g)])
+        load_words(xw[:, A, xcols(1)], xa_words[:, :, xcols(1)])
+        load_words(xw[:, B, xcols(1)], xb_words[:, :, xcols(1)])
+        eps_r = eps.rearrange("(s p) n -> p s n", p=P)
+        nc.sync.dma_start(out=eps_sb[:, 0:4, :], in_=eps_r[:, 0:4, :])
+        nc.sync.dma_start(out=eps_sb[:, 4:8, :], in_=eps_r[:, 4:8, :])
+        for words, first, last in ((da_words, 0, 2048), (db_words, 2048, 3072)):
+            rows = words.bitcast(I32).rearrange("g p n -> (g p) n").rearrange("(i e a) n -> i a e n", e=E, a=32)
+            for i in range(4):
+                nc.sync.dma_start(out=dw[32 * i : 32 * (i + 1), :, first:last].bitcast(I32), in_=rows[i])
+        for scales, first, last in ((da_scales, 0, 1024), (db_scales, 1024, 1536)):
+            rows = scales.bitcast(I32).rearrange("g q n -> (g q) n").rearrange("(i e r) n -> r i e n", e=E, r=4)
+            for r in range(4):
+                nc.sync.dma_start(out=dsc[r:P:32, :, first:last].bitcast(I32), in_=rows[r])
+        nc.sync.dma_start(out=cbb[:], in_=cb.partition_broadcast(P))
+        nc.sync.dma_start(out=cab2[:], in_=ca[512:1024].partition_broadcast(P))
+
+        def turn_rows(rows, vecs, n, b):
+            full = work.tile([P, P], F32, name="full")
+            nc.vector.tensor_copy(out=full[:], in_=rows[:])
+            nc.tensor.transpose(b[:, 0:P], full[:], ident[:])
+            nc.vector.tensor_copy(out=vecs[:], in_=b[:, 0:n])
+
+        def encode(dst, c, j, h, ks):
+            for n, k in enumerate(ks):
+                col = c * N + P * j
+                nc.tensor.matmul_mx(
+                    out=dst[:],
+                    lhsT=ww[:, k, 2 * col : 2 * (col + P)].bitcast(FP4X4),
+                    lhsT_scale=ws[:, k, col : col + P],
+                    rhs=xw[:, k, xcols(h)].bitcast(FP4X4),
+                    rhs_scale=xs[:, k, h * HALF : (h + 1) * HALF],
+                    start=(n == 0),
+                    stop=(n == len(ks) - 1),
+                )
+
+        def unit(h, j, ks, hook=None):
+            la, lb, ma, mb = [bank(k) for k in ks]
+            encode(la, 1, j, h, (0, 1))
+            if hook:
+                hook()
+            encode(lb, 1, j, h, (2,))
+            encode(ma, 0, j, h, (0, 1))
+            encode(mb, 0, j, h, (2,))
+            ta = work.tile([P, HALF], F32, name="ta")
+            tb = work.tile([P, HALF], F32, name="tb")
+            u = work.tile([P, HALF], F32, name="u")
+            v = work.tile([P, HALF], F32, name="v")
+            nc.scalar.activation(out=ta[:], in_=la[:], func=ACT.Exp, bias=v1[:, NT + j : NT + j + 1])
+            nc.scalar.activation(out=tb[:], in_=lb[:], func=ACT.Exp, bias=v1[:, 3 * NT + j : 3 * NT + j + 1])
+            nc.vector.scalar_tensor_tensor(out=u[:], in0=ma[:], scalar=v1[:, j : j + 1], in1=ta[:], op0=ALU.add, op1=ALU.mult)
+            nc.vector.scalar_tensor_tensor(out=v[:], in0=mb[:], scalar=v1[:, 2 * NT + j : 2 * NT + j + 1], in1=tb[:], op0=ALU.add, op1=ALU.mult)
+            nc.gpsimd.tensor_tensor(out=lam[:, h, j, :], in0=ta[:], in1=tb[:], op=ALU.add)
+            return (h, j, u, v)
+
+        def w(un, eng):
+            h, j, u, v = un
+            eng.tensor_tensor(out=num[:, h, j, :], in0=u[:], in1=v[:], op=ALU.add)
+
+        def rsqrt(h, j):
+            nc.scalar.activation(out=lam[:, h, j, :], in_=lam[:, h, j, :], func=ACT.Abs_reciprocal_sqrt, bias=t0[:, j : j + 1])
+
+        def turn_eps(h, i, k):
+            b = bank(k, BF16)
+            for e in range(E):
+                for s in range(4):
+                    first = HALF * e + P * s
+                    nc.tensor.transpose(b[:, first : first + P], eps_sb[:, 4 * h + s, P * (2 * i + e) : P * (2 * i + e + 1)], identb[:])
+            return b
+
+        def z_m(h, j):
+            nc.vector.scalar_tensor_tensor(
+                out=num[:, h, j, :], in0=num[:, h, j, :], scalar=c0[:, j : j + 1], in1=lam[:, h, j, :], op0=ALU.add, op1=ALU.mult
+            )
+
+        def flat(t, h, i):
+            return t[:, h, 2 * i : 2 * i + 2, :].rearrange("p j s -> p (j s)")
+
+        def z_t(h, i, b):
+            nc.vector.tensor_tensor(out=flat(num, h, i), in0=flat(num, h, i), in1=b[:], op=ALU.add)
+
+        def z_z(h, i, zd, eng):
+            zb = work.tile([P, E, HALF], BF16, align_bytes=64, name="zb")
+            eng.tensor_tensor(out=zb[:].rearrange("p e s -> p (e s)"), in0=flat(num, h, i), in1=flat(lam, h, i), op=ALU.mult)
+            for t in range(T):
+                nc.sync.dma_start(out=zd[32 * i : 32 * (i + 1), t, :, :], in_=zb[t:P:4, :, :])
+
+        def z_i(e, zd, eng):
+            zi = twice.tile([P, HALF * T], BF16, align_bytes=64, name="zi")
+            src = zd[:, :, e, :].rearrange("p t (c i) -> p c t i", i=4)
+            dst = zi[:].rearrange("p (c i t) -> p c t i", i=4, t=T)
+            if eng == "S":
+                nc.scalar.copy(out=dst, in_=src)
+            else:
+                nc.vector.tensor_copy(out=dst, in_=src)
+            return zi
+
+        def z_q(h, e, zi):
+            cols = slice(h * HALF, (h + 1) * HALF)
+            nc.vector.quantize_mx(out=zq[:, e, cols].bitcast(FP8X4), scales=zs[:, e, cols], in_=zi[:])
+
+        def decode_t(f, s0, ns, b):
+            n = P * ns if ns == 4 else P
+            for c in range(P * ns // n):
+                cols = slice(s0 * P + c * n, s0 * P + (c + 1) * n)
+                for e in range(E):
+                    nc.tensor.matmul_mx(
+                        out=b[:, c * n : (c + 1) * n],
+                        lhsT=dw[:, e, 256 * f : 256 * (f + 1)].bitcast(FP4X4),
+                        lhsT_scale=dsc[:, e, P * f : P * (f + 1)],
+                        rhs=zq[:, e, cols].bitcast(FP8X4),
+                        rhs_scale=zs[:, e, cols],
+                        start=(e == 0),
+                        stop=(e == E - 1),
+                    )
+
+        def decode(s, first, b):
+            cols = slice(s * P, (s + 1) * P)
+            for e in range(E):
+                nc.tensor.matmul_mx(
+                    out=b[:],
+                    lhsT=zq[:, e, cols].bitcast(FP8X4),
+                    lhsT_scale=zs[:, e, cols],
+                    rhs=dw[:, e, 2 * first : 2 * (first + 512)].bitcast(FP4X4),
+                    rhs_scale=dsc[:, e, first : first + 512],
+                    start=(e == 0),
+                    stop=(e == E - 1),
+                )
+
+        out_ar = out_a.rearrange("(s p) n -> p s n", p=P)
+        out_br = out_b.rearrange("(s p) n -> p s n", p=P)
+
+        def direct(s, blk, k):
+            b = bank(k)
+            decode(s, 512 * blk, b)
+            yd = outs.tile([P, 512], F32, name="yd")
+            bias = cbb if blk == 2 else cab2
+            nc.vector.tensor_tensor(out=yd[:], in0=b[:], in1=bias[:], op=ALU.add)
+            dst = out_b[s * P : (s + 1) * P, :] if blk == 2 else out_a[s * P : (s + 1) * P, 512:1024]
+            nc.sync.dma_start(out=dst, in_=yd[:])
+
+        def acc(f, s0, ns, b):
+            decode_t(f, s0, ns, b)
+            yt = outs.tile([P, HALF], F32, name="yt")
+            nc.scalar.activation(out=yt[:, 0 : P * ns], in_=b[:, 0 : P * ns], func=ACT.Identity, bias=v2[:, 16 + f : 17 + f])
+            return yt
+
+        def turn(f, ns, yt, b, yo):
+            for s in range(ns):
+                nc.tensor.transpose(b[:, P * s : P * (s + 1)], yt[:, P * s : P * (s + 1)], ident[:])
+            q = f % 4
+            nc.scalar.copy(out=yo[:, 0:ns, P * q : P * (q + 1)], in_=b[:, 0 : P * ns].rearrange("p (s n) -> p s n", s=ns))
+
+        def store(f, s0, ns, yo, q0, q1):
+            dst = (out_br if f >= 8 else out_ar)[:, s0 : s0 + ns, (f // 4 % 2) * 512 + P * q0 : (f // 4 % 2) * 512 + P * q1]
+            nc.sync.dma_start(out=dst, in_=yo[:, 0:ns, P * q0 : P * q1])
+
+        def run(s0, ns, fs, accs, turns, hook=lambda n: None):
+            prev = None
+            yo = None
+            for n, f in enumerate(fs):
+                if f % 4 == 0:
+                    nxt = outs.tile([P, 4, 512], F32, name="yo")
+                yt = acc(f, s0, ns, bank(accs[n % len(accs)]))
+                if prev is not None:
+                    turn(prev[0], ns, prev[1], bank(turns[(n - 1) % len(turns)]), prev[2])
+                    if prev[0] % 2 == 1:
+                        store(prev[0], s0, ns, prev[2], prev[0] % 4 - 1, prev[0] % 4 + 1)
+                prev = (f, yt, nxt)
+                hook(n)
+            turn(prev[0], ns, prev[1], bank(turns[(len(fs) - 1) % len(turns)]), prev[2])
+            store(prev[0], s0, ns, prev[2], prev[0] % 4 - 1, prev[0] % 4 + 1)
+
+        V, G = nc.vector, nc.gpsimd
+        eb = {}
+        zd = {}
+        zi = {}
+
+        def eps_(h, i, k):
+            eb[h, i] = turn_eps(h, i, k)
+
+        def zt(h, i):
+            z_t(h, i, eb[h, i])
+
+        def zz(h, i, eng):
+            if h not in zd:
+                zd[h] = twice.tile([P, T, E, HALF], BF16, align_bytes=64, name="zd")
+            z_z(h, i, zd[h], eng)
+
+        def inter(h, e, eng):
+            zi[h, e] = z_i(e, zd[h], eng)
+
+        def quant(h, e):
+            z_q(h, e, zi[h, e])
+
+        def m2(h, i):
+            z_m(h, 2 * i)
+            z_m(h, 2 * i + 1)
+
+        dn = [0]
+
+        def dir_(s, blk):
+            direct(s, blk, (4, 5)[dn[0] % 2])
+            dn[0] += 1
+
+        prev = None
+        for i in range(8):
+            now = unit(0, i, [4 * (i % 2) + b for b in range(4)], (lambda: turn_rows(rows1, v1, 32, bank(7))) if i == 0 else None)
+            if prev is not None:
+                w(prev, G if i % 3 == 0 else V)
+            prev = now
+            if i == 5:
+                nc.vector.tensor_copy(out=identb[:], in_=ident[:])
+                turn_rows(rows2, v2, 28, bank(3))
+                nc.scalar.activation(out=t0[:], in_=v2[:, 0:8], func=ACT.Exp)
+                nc.vector.tensor_tensor(out=c0[:], in0=t0[:], in1=v2[:, 8:16], op=ALU.mult)
+        w(prev, G)
+
+        def u1(j):
+            k = 2 + 2 * (j % 2)
+            w(unit(1, j, (0, 1, k, k + 1)), G)
+
+        u1(0)
+        eps_(0, 0, 6)
+        eps_(0, 1, 7)
+        for j in range(8):
+            rsqrt(0, j)
+        m2(0, 0)
+        m2(0, 1)
+        zt(0, 0)
+        u1(1)
+        zt(0, 1)
+        zz(0, 0, V)
+        eps_(0, 2, 6)
+        u1(2)
+        zz(0, 1, V)
+        eps_(0, 3, 7)
+        m2(0, 2)
+        u1(3)
+        m2(0, 3)
+        zt(0, 2)
+        u1(4)
+        zt(0, 3)
+        zz(0, 2, V)
+        eps_(1, 0, 6)
+        u1(5)
+        zz(0, 3, V)
+        eps_(1, 1, 7)
+        u1(6)
+        u1(7)
+        inter(0, 0, "S")
+        for j in range(8):
+            rsqrt(1, j)
+        inter(0, 1, "S")
+        m2(1, 0)
+        quant(0, 0)
+        m2(1, 1)
+        zt(1, 0)
+        zt(1, 1)
+        zz(1, 0, G)
+        eps_(1, 2, 6)
+        eps_(1, 3, 7)
+        quant(0, 1)
+        m2(1, 2)
+        zz(1, 1, V)
+        zt(1, 2)
+        m2(1, 3)
+        zz(1, 2, V)
+        zt(1, 3)
+
+        def hook0(n):
+            if n == 0:
+                dir_(0, 2)
+                zz(1, 3, V)
+                dir_(0, 1)
+            elif n < 4:
+                dir_(n, 2)
+                dir_(n, 1)
+            if n == 3:
+                inter(1, 0, "S")
+                inter(1, 1, "V")
+                quant(1, 0)
+                quant(1, 1)
+        run(0, 4, list(range(4)), (0, 2), (1, 3), hook0)
+
+        def hook1(n):
+            dir_(4 + n, 1)
+            dir_(4 + n, 2)
+        run(4, 4, list(range(4)), (0, 2), (1, 3), hook1)

@@ -36,7 +36,7 @@ def tile_product_of_experts_fusion_f2_kernel(
         twice = ctx.enter_context(tc.tile_pool(name="twice", bufs=2))
         outs = ctx.enter_context(tc.tile_pool(name="outs", bufs=3))
         psum = ctx.enter_context(tc.psum_pool(name="psum", bufs=1))
-        ctx.enter_context(tc.manual_schedule())
+        ctx.enter_context(tc.manual_schedule(engines={mybir.EngineType.Activation, mybir.EngineType.SP}))
 
         def bank(i, dt=F32):
             return psum.tile([P, 2048 // (4 if dt == F32 else 2)], dt, tag="b%d" % i, name="b%d" % i)
@@ -53,7 +53,6 @@ def tile_product_of_experts_fusion_f2_kernel(
         zq = keep.tile([P, E, M], U32, align_bytes=64, name="zq")
         zs = keep.tile([P, E, M], U8, align_bytes=64, name="zs")
         ident = keep.tile([P, P], F32, align_bytes=64, name="ident")
-        identb = keep.tile([P, P], BF16, align_bytes=64, name="identb")
         warm = keep.tile([P, 1], F32, name="warm")
         warm2 = keep.tile([P, 1], F32, name="warm2")
         rows1 = keep.tile([P, P], BF16, name="rows1")
@@ -70,7 +69,6 @@ def tile_product_of_experts_fusion_f2_kernel(
             nc.gpsimd.memset(xs[:, k, :].rearrange("p a n -> p (a n)").bitcast(I32), 0)
             nc.vector.memset(ws[:, k, :].rearrange("p a n -> p (a n)").bitcast(I32), 0)
         nc.gpsimd.memset(rows1[:], 0.0)
-        nc.scalar.activation(out=warm2[:], in_=warm[:], func=ACT.Exp)
 
         def load_scales(engs, plane, groups, cols, src):
             for r in range(4):
@@ -93,12 +91,13 @@ def tile_product_of_experts_fusion_f2_kernel(
 
         load_words(ww[:, A, wcols(1, 0)], wa_words[:, :, wcols(1, 0)])
         load_words(xw[:, A, xcols(0)], xa_words[:, :, xcols(0)])
-        load_scales([nc.scalar] * 4, xs, A, slice(0, M), xa_scales)
-        load_scales([nc.scalar, nc.scalar, nc.gpsimd, nc.gpsimd], ws, A, slice(0, 2 * N), wa_scales)
+        load_scales([nc.sync] * 4, xs, A, slice(0, M), xa_scales)
+        load_scales([nc.scalar] * 4, ws, A, slice(0, 2 * N), wa_scales)
+        nc.scalar.activation(out=warm2[:], in_=warm[:], func=ACT.Exp)
         load_words(ww[:, B, wcols(1, 0)], wb_words[:, :, wcols(1, 0)])
         load_words(xw[:, B, xcols(0)], xb_words[:, :, xcols(0)])
-        load_scales([nc.scalar] * 4, xs, B, slice(0, M), xb_scales)
-        load_scales([nc.scalar] * 4, ws, B, slice(0, 2 * N), wb_scales)
+        load_scales([nc.sync] * 4, xs, B, slice(0, M), xb_scales)
+        load_scales([nc.sync] * 4, ws, B, slice(0, 2 * N), wb_scales)
         nc.gpsimd.dma_start(out=rows1[0:16, :], in_=ba.rearrange("(c p) -> c p", p=P))
         nc.gpsimd.dma_start(out=rows1[16:32, :], in_=bb.rearrange("(c p) -> c p", p=P))
         make_identity(nc, ident[:])
@@ -116,14 +115,10 @@ def tile_product_of_experts_fusion_f2_kernel(
         eps_r = eps.rearrange("(s p) n -> p s n", p=P)
         nc.sync.dma_start(out=eps_sb[:, 0:4, :], in_=eps_r[:, 0:4, :])
         nc.sync.dma_start(out=eps_sb[:, 4:8, :], in_=eps_r[:, 4:8, :])
-        for words, first, last in ((da_words, 0, 2048), (db_words, 2048, 3072)):
-            rows = words.bitcast(I32).rearrange("g p n -> (g p) n").rearrange("(i e a) n -> i a e n", e=E, a=32)
-            for i in range(4):
-                nc.sync.dma_start(out=dw[32 * i : 32 * (i + 1), :, first:last].bitcast(I32), in_=rows[i])
-        for scales, first, last in ((da_scales, 0, 1024), (db_scales, 1024, 1536)):
-            rows = scales.bitcast(I32).rearrange("g q n -> (g q) n").rearrange("(i e r) n -> r i e n", e=E, r=4)
-            for r in range(4):
-                nc.sync.dma_start(out=dsc[r:P:32, :, first:last].bitcast(I32), in_=rows[r])
+        load_words(dw[:, :, 0:2048], da_words)
+        load_words(dw[:, :, 2048:3072], db_words)
+        load_scales([nc.sync] * 4, dsc, slice(0, E), slice(0, 1024), da_scales)
+        load_scales([nc.sync] * 4, dsc, slice(0, E), slice(1024, 1536), db_scales)
         nc.sync.dma_start(out=cbb[:], in_=cb.partition_broadcast(P))
         nc.sync.dma_start(out=cab2[:], in_=ca[512:1024].partition_broadcast(P))
 
@@ -172,44 +167,48 @@ def tile_product_of_experts_fusion_f2_kernel(
         def rsqrt(h, j):
             nc.scalar.activation(out=lam[:, h, j, :], in_=lam[:, h, j, :], func=ACT.Abs_reciprocal_sqrt, bias=t0[:, j : j + 1])
 
-        def turn_eps(h, i, k):
-            b = bank(k, BF16)
-            for e in range(E):
-                for s in range(4):
-                    first = HALF * e + P * s
-                    nc.tensor.transpose(b[:, first : first + P], eps_sb[:, 4 * h + s, P * (2 * i + e) : P * (2 * i + e + 1)], identb[:])
-            return b
-
         def z_m(h, j):
             nc.vector.scalar_tensor_tensor(
                 out=num[:, h, j, :], in0=num[:, h, j, :], scalar=c0[:, j : j + 1], in1=lam[:, h, j, :], op0=ALU.add, op1=ALU.mult
             )
 
-        def flat(t, h, i):
-            return t[:, h, 2 * i : 2 * i + 2, :].rearrange("p j s -> p (j s)")
+        def turn_item(s, g, km, kr):
+            h, sl = divmod(s, 4)
+            bm, br = bank(km), bank(kr)
+            for b, src in ((bm, num), (br, lam)):
+                for jj in range(4):
+                    nc.tensor.transpose(b[:, P * jj : P * (jj + 1)], src[:, h, 4 * g + jj, P * sl : P * (sl + 1)], ident[:])
+            return bm, br
 
-        def z_t(h, i, b):
-            nc.vector.tensor_tensor(out=flat(num, h, i), in0=flat(num, h, i), in1=b[:], op=ALU.add)
+        def z_t(s, g, bm):
+            zt = work.tile([P, 512], F32, name="zt")
+            nc.vector.tensor_tensor(out=zt[:], in0=bm[:], in1=eps_sb[:, s, 512 * g : 512 * (g + 1)], op=ALU.add)
+            return zt
 
-        def z_z(h, i, zd, eng):
-            zb = work.tile([P, E, HALF], BF16, align_bytes=64, name="zb")
-            eng.tensor_tensor(out=zb[:].rearrange("p e s -> p (e s)"), in0=flat(num, h, i), in1=flat(lam, h, i), op=ALU.mult)
-            for t in range(T):
-                nc.sync.dma_start(out=zd[32 * i : 32 * (i + 1), t, :, :], in_=zb[t:P:4, :, :])
+        def z_z(zt, br):
+            zb = work.tile([P, 512], BF16, align_bytes=64, name="zb")
+            nc.vector.tensor_tensor(out=zb[:], in0=br[:], in1=zt[:], op=ALU.mult)
+            return zb
 
-        def z_i(e, zd, eng):
-            zi = twice.tile([P, HALF * T], BF16, align_bytes=64, name="zi")
-            src = zd[:, :, e, :].rearrange("p t (c i) -> p c t i", i=4)
-            dst = zi[:].rearrange("p (c i t) -> p c t i", i=4, t=T)
+        def turn_words(s, zb, b):
+            words = zb[:].bitcast(F32)
+            for u in range(2):
+                first = 256 * u + P * (s % 2)
+                nc.tensor.transpose(b[:, first : first + P], words[:, u : u + 255 : 2], ident[:])
+
+        def z_x(b, eng):
+            zi = twice.tile([P, 256 * T], BF16, align_bytes=64, name="zi")
+            dst = zi[:].bitcast(F32).rearrange("p (c i u) -> p c u i", i=4, u=2)
+            src = b[:].rearrange("p (u c i) -> p c u i", i=4, u=2)
             if eng == "S":
                 nc.scalar.copy(out=dst, in_=src)
             else:
                 nc.vector.tensor_copy(out=dst, in_=src)
             return zi
 
-        def z_q(h, e, zi):
-            cols = slice(h * HALF, (h + 1) * HALF)
-            nc.vector.quantize_mx(out=zq[:, e, cols].bitcast(FP8X4), scales=zs[:, e, cols], in_=zi[:])
+        def z_q(sp, g, zi):
+            cols = slice(sp * 256, (sp + 1) * 256)
+            nc.vector.quantize_mx(out=zq[:, g, cols].bitcast(FP8X4), scales=zs[:, g, cols], in_=zi[:])
 
         def decode_t(f, s0, ns, b):
             n = P * ns if ns == 4 else P
@@ -271,7 +270,7 @@ def tile_product_of_experts_fusion_f2_kernel(
             prev = None
             yo = None
             for n, f in enumerate(fs):
-                if f % 4 == 0:
+                if n == 0 or f % 4 == 0:
                     nxt = outs.tile([P, 4, 512], F32, name="yo")
                 yt = acc(f, s0, ns, bank(accs[n % len(accs)]))
                 if prev is not None:
@@ -284,118 +283,143 @@ def tile_product_of_experts_fusion_f2_kernel(
             store(prev[0], s0, ns, prev[2], prev[0] % 4 - 1, prev[0] % 4 + 1)
 
         V, G = nc.vector, nc.gpsimd
-        eb = {}
-        zd = {}
+        it = {}
         zi = {}
+        wb = {}
 
-        def eps_(h, i, k):
-            eb[h, i] = turn_eps(h, i, k)
+        def m4(h, g):
+            for j in range(4 * g, 4 * g + 4):
+                z_m(h, j)
 
-        def zt(h, i):
-            z_t(h, i, eb[h, i])
+        def r4(h, g):
+            for j in range(4 * g, 4 * g + 4):
+                rsqrt(h, j)
 
-        def zz(h, i, eng):
-            if h not in zd:
-                zd[h] = twice.tile([P, T, E, HALF], BF16, align_bytes=64, name="zd")
-            z_z(h, i, zd[h], eng)
+        def ti(s, g, km, kr):
+            it[s, g] = list(turn_item(s, g, km, kr))
 
-        def inter(h, e, eng):
-            zi[h, e] = z_i(e, zd[h], eng)
+        def tz(*items):
+            for i in items:
+                it[i].append(z_t(*i, it[i][0]))
+            for i in items:
+                it[i].append(z_z(it[i][2], it[i][1]))
 
-        def quant(h, e):
-            z_q(h, e, zi[h, e])
+        def wd(s, g, k):
+            if s % 2 == 0:
+                wb[s // 2, g] = bank(k)
+            turn_words(s, it[s, g][3], wb[s // 2, g])
 
-        def m2(h, i):
-            z_m(h, 2 * i)
-            z_m(h, 2 * i + 1)
+        def xx(sp, g, eng="S"):
+            zi[sp, g] = z_x(wb[sp, g], eng)
+
+        def qq(sp, g):
+            z_q(sp, g, zi[sp, g])
 
         dn = [0]
 
-        def dir_(s, blk):
-            direct(s, blk, (4, 5)[dn[0] % 2])
+        def dir_(s, blk, ks=(4, 5)):
+            direct(s, blk, ks[dn[0] % len(ks)])
             dn[0] += 1
 
         prev = None
         for i in range(8):
             now = unit(0, i, [4 * (i % 2) + b for b in range(4)], (lambda: turn_rows(rows1, v1, 32, bank(7))) if i == 0 else None)
             if prev is not None:
-                w(prev, G if i % 3 == 0 else V)
+                w(prev, G if i % 3 else V)
             prev = now
             if i == 5:
-                nc.vector.tensor_copy(out=identb[:], in_=ident[:])
                 turn_rows(rows2, v2, 28, bank(3))
                 nc.scalar.activation(out=t0[:], in_=v2[:, 0:8], func=ACT.Exp)
                 nc.vector.tensor_tensor(out=c0[:], in0=t0[:], in1=v2[:, 8:16], op=ALU.mult)
         w(prev, G)
 
         def u1(j):
-            k = 2 + 2 * (j % 2)
-            w(unit(1, j, (0, 1, k, k + 1)), G)
+            w(unit(1, j, (0, 1, 2, 3)), G)
 
         u1(0)
-        eps_(0, 0, 6)
-        eps_(0, 1, 7)
-        for j in range(8):
-            rsqrt(0, j)
-        m2(0, 0)
-        m2(0, 1)
-        zt(0, 0)
+        r4(0, 0)
+        r4(0, 1)
+        m4(0, 0)
+        ti(0, 0, 4, 5)
+        ti(1, 0, 6, 7)
         u1(1)
-        zt(0, 1)
-        zz(0, 0, V)
-        eps_(0, 2, 6)
+        m4(0, 1)
+        tz((0, 0), (1, 0))
+        ti(0, 1, 4, 5)
         u1(2)
-        zz(0, 1, V)
-        eps_(0, 3, 7)
-        m2(0, 2)
+        wd(0, 0, 6)
+        wd(1, 0, 6)
+        xx(0, 0)
+        tz((0, 1))
         u1(3)
-        m2(0, 3)
-        zt(0, 2)
+        ti(1, 1, 4, 5)
+        tz((1, 1))
+        wd(0, 1, 7)
+        wd(1, 1, 7)
+        xx(0, 1)
         u1(4)
-        zt(0, 3)
-        zz(0, 2, V)
-        eps_(1, 0, 6)
+        ti(2, 0, 4, 5)
+        qq(0, 0)
+        tz((2, 0))
+        qq(0, 1)
         u1(5)
-        zz(0, 3, V)
-        eps_(1, 1, 7)
+        ti(3, 0, 4, 5)
+        tz((3, 0))
+        wd(2, 0, 6)
+        wd(3, 0, 6)
+        xx(1, 0)
         u1(6)
+        ti(2, 1, 4, 5)
+        tz((2, 1))
+        qq(1, 0)
         u1(7)
-        inter(0, 0, "S")
-        for j in range(8):
-            rsqrt(1, j)
-        inter(0, 1, "S")
-        m2(1, 0)
-        quant(0, 0)
-        m2(1, 1)
-        zt(1, 0)
-        zt(1, 1)
-        zz(1, 0, G)
-        eps_(1, 2, 6)
-        eps_(1, 3, 7)
-        quant(0, 1)
-        m2(1, 2)
-        zz(1, 1, V)
-        zt(1, 2)
-        m2(1, 3)
-        zz(1, 2, V)
-        zt(1, 3)
-
-        def hook0(n):
-            if n == 0:
-                dir_(0, 2)
-                zz(1, 3, V)
-                dir_(0, 1)
-            elif n < 4:
-                dir_(n, 2)
-                dir_(n, 1)
-            if n == 3:
-                inter(1, 0, "S")
-                inter(1, 1, "V")
-                quant(1, 0)
-                quant(1, 1)
-        run(0, 4, list(range(4)), (0, 2), (1, 3), hook0)
-
-        def hook1(n):
-            dir_(4 + n, 1)
-            dir_(4 + n, 2)
-        run(4, 4, list(range(4)), (0, 2), (1, 3), hook1)
+        ti(3, 1, 4, 5)
+        tz((3, 1))
+        wd(2, 1, 7)
+        wd(3, 1, 7)
+        xx(1, 1)
+        r4(1, 0)
+        r4(1, 1)
+        dir_(0, 2, (0, 1))
+        dir_(0, 1, (0, 1))
+        dir_(1, 2, (0, 1))
+        dir_(1, 1, (0, 1))
+        m4(1, 0)
+        ti(4, 0, 4, 5)
+        ti(5, 0, 6, 7)
+        qq(1, 1)
+        m4(1, 1)
+        tz((4, 0), (5, 0))
+        ti(4, 1, 4, 5)
+        ti(5, 1, 6, 7)
+        run(0, 4, [0, 1], (2,), (3,))
+        wd(4, 0, 0)
+        wd(5, 0, 0)
+        xx(2, 0)
+        tz((4, 1), (5, 1))
+        wd(4, 1, 1)
+        wd(5, 1, 1)
+        xx(2, 1)
+        ti(6, 0, 4, 5)
+        ti(7, 0, 6, 7)
+        run(0, 4, [2, 3], (2,), (3,))
+        dir_(2, 2, (2, 3))
+        qq(2, 0)
+        tz((6, 0), (7, 0))
+        dir_(2, 1, (2, 3))
+        qq(2, 1)
+        ti(6, 1, 4, 5)
+        ti(7, 1, 6, 7)
+        wd(6, 0, 0)
+        wd(7, 0, 0)
+        xx(3, 0)
+        tz((6, 1), (7, 1))
+        wd(6, 1, 1)
+        wd(7, 1, 1)
+        xx(3, 1)
+        dir_(3, 2, (2, 3))
+        qq(3, 0)
+        dir_(3, 1, (2, 3))
+        qq(3, 1)
+        run(4, 2, [0, 1, 2, 3], (4, 5), (6, 7), lambda n: dir_(4 + n // 2, 1 + n % 2, (2, 3)))
+        run(6, 2, [0, 1, 2, 3], (4, 5), (6, 7), lambda n: dir_(6 + n // 2, 1 + n % 2, (0, 1)))

@@ -45,6 +45,8 @@ def tile_product_of_experts_fusion_f2_kernel(
         xs = keep.tile([P, KG, M], U8, align_bytes=64, name="xs")
         ww = keep.tile([P, KG, 4 * N], U8, align_bytes=64, name="ww")
         ws = keep.tile([P, KG, 2 * N], U8, align_bytes=64, name="ws")
+        wp = keep.tile([P, 2, E, KG, 1024], U8, align_bytes=64, name="wp")
+        wsp = keep.tile([P, 2, E, KG, 512], U8, align_bytes=64, name="wsp")
         dw = keep.tile([P, E, 3072], U8, align_bytes=64, name="dw")
         dsc = keep.tile([P, E, 1536], U8, align_bytes=64, name="dsc")
         eps_sb = keep.tile([P, 8, N], BF16, align_bytes=64, name="eps_sb")
@@ -55,20 +57,25 @@ def tile_product_of_experts_fusion_f2_kernel(
         ident = keep.tile([P, P], F32, align_bytes=64, name="ident")
         warm = keep.tile([P, 1], F32, name="warm")
         warm2 = keep.tile([P, 1], F32, name="warm2")
-        rows1 = keep.tile([P, P], BF16, name="rows1")
         rows2 = keep.tile([P, P], BF16, name="rows2")
-        v1 = keep.tile([P, 32], F32, name="v1")
-        v2 = keep.tile([P, 28], F32, name="v2")
+        v2 = keep.tile([P, 12], F32, name="v2")
         t0 = keep.tile([P, NT], F32, name="t0")
         c0 = keep.tile([P, NT], F32, name="c0")
-        cbb = keep.tile([P, KB], BF16, name="cbb")
-        cab2 = keep.tile([P, HALF], BF16, name="cab2")
+        ball = keep.tile([P, KA + KB], BF16, name="ball")
 
-        nc.vector.memset(warm[:], 0.0)
         for k in (slice(0, GA), slice(GA, KG)):
-            nc.gpsimd.memset(xs[:, k, :].rearrange("p a n -> p (a n)").bitcast(I32), 0)
+            nc.vector.memset(xs[:, k, :].rearrange("p a n -> p (a n)").bitcast(I32), 0)
             nc.vector.memset(ws[:, k, :].rearrange("p a n -> p (a n)").bitcast(I32), 0)
-        nc.gpsimd.memset(rows1[:], 0.0)
+        nc.vector.memset(warm[:], 0.0)
+        va = keep.tile([P, 4, T], BF16, name="va")
+        vb = keep.tile([P, 4, T], BF16, name="vb")
+        vm = keep.tile([P, E, T], BF16, name="vm")
+        vl = keep.tile([P, E, T], BF16, name="vl")
+        fa = keep.tile([P, 4 * T], F32, name="fa")
+        fb = keep.tile([P, 4 * T], F32, name="fb")
+        nc.gpsimd.dma_start(out=va[:], in_=ba.rearrange("(c p t) -> p c t", p=P, t=T))
+        nc.gpsimd.dma_start(out=vb[:], in_=bb.rearrange("(c p t) -> p c t", p=P, t=T))
+        make_identity(nc, ident[:])
 
         def load_scales(engs, plane, groups, cols, src):
             for r in range(4):
@@ -98,15 +105,12 @@ def tile_product_of_experts_fusion_f2_kernel(
         load_words(xw[:, B, xcols(0)], xb_words[:, :, xcols(0)])
         load_scales([nc.sync] * 4, xs, B, slice(0, M), xb_scales)
         load_scales([nc.sync] * 4, ws, B, slice(0, 2 * N), wb_scales)
-        nc.gpsimd.dma_start(out=rows1[0:16, :], in_=ba.rearrange("(c p) -> c p", p=P))
-        nc.gpsimd.dma_start(out=rows1[16:32, :], in_=bb.rearrange("(c p) -> c p", p=P))
-        make_identity(nc, ident[:])
         nc.gpsimd.memset(dsc[:].rearrange("p a n -> p (a n)").bitcast(I32), 0)
         nc.gpsimd.memset(rows2[:], 0.0)
-        nc.gpsimd.dma_start(out=rows2[0:8, :], in_=prior_logprec.rearrange("(c p) -> c p", p=P))
-        nc.gpsimd.dma_start(out=rows2[8:16, :], in_=prior_mean.rearrange("(c p) -> c p", p=P))
-        nc.gpsimd.dma_start(out=rows2[16:24, :], in_=ca.rearrange("(c p) -> c p", p=P))
-        nc.gpsimd.dma_start(out=rows2[24:28, :], in_=cb.rearrange("(c p) -> c p", p=P))
+        nc.gpsimd.dma_start(out=vl[:], in_=prior_logprec.rearrange("(c p t) -> p c t", p=P, t=T))
+        nc.gpsimd.dma_start(out=vm[:], in_=prior_mean.rearrange("(c p t) -> p c t", p=P, t=T))
+        nc.gpsimd.dma_start(out=rows2[0:8, :], in_=ca.rearrange("(c p) -> c p", p=P))
+        nc.gpsimd.dma_start(out=rows2[8:12, :], in_=cb.rearrange("(c p) -> c p", p=P))
         for c, g in ((0, 0), (1, 1), (0, 1)):
             load_words(ww[:, A, wcols(c, g)], wa_words[:, :, wcols(c, g)])
             load_words(ww[:, B, wcols(c, g)], wb_words[:, :, wcols(c, g)])
@@ -119,8 +123,20 @@ def tile_product_of_experts_fusion_f2_kernel(
         load_words(dw[:, :, 2048:3072], db_words)
         load_scales([nc.sync] * 4, dsc, slice(0, E), slice(0, 1024), da_scales)
         load_scales([nc.sync] * 4, dsc, slice(0, E), slice(1024, 1536), db_scales)
-        nc.sync.dma_start(out=cbb[:], in_=cb.partition_broadcast(P))
-        nc.sync.dma_start(out=cab2[:], in_=ca[512:1024].partition_broadcast(P))
+        nc.sync.dma_start(out=ball[:, 0:KA], in_=ca.partition_broadcast(P))
+        nc.sync.dma_start(out=ball[:, KA : KA + KB], in_=cb.partition_broadcast(P))
+
+        def perm_words(c, g, k):
+            nc.vector.tensor_copy(
+                out=wp[:, c, g, k, :].rearrange("p (t m b) -> p t m b", t=T, b=2),
+                in_=ww[:, k, wcols(c, g)].rearrange("p (m t b) -> p t m b", t=T, b=2),
+            )
+
+        def perm_scales(c, g, ks):
+            nc.vector.tensor_copy(
+                out=wsp[:, c, g, ks, :].rearrange("p k (t m) -> p k t m", t=T),
+                in_=ws[:, ks, c * N + g * 512 : c * N + (g + 1) * 512].rearrange("p k (m t) -> p k t m", t=T),
+            )
 
         def turn_rows(rows, vecs, n, b):
             full = work.tile([P, P], F32, name="full")
@@ -130,11 +146,11 @@ def tile_product_of_experts_fusion_f2_kernel(
 
         def encode(dst, c, j, h, ks):
             for n, k in enumerate(ks):
-                col = c * N + P * j
+                g, t = divmod(j, T)
                 nc.tensor.matmul_mx(
                     out=dst[:],
-                    lhsT=ww[:, k, 2 * col : 2 * (col + P)].bitcast(FP4X4),
-                    lhsT_scale=ws[:, k, col : col + P],
+                    lhsT=wp[:, c, g, k, 256 * t : 256 * (t + 1)].bitcast(FP4X4),
+                    lhsT_scale=wsp[:, c, g, k, P * t : P * (t + 1)],
                     rhs=xw[:, k, xcols(h)].bitcast(FP4X4),
                     rhs_scale=xs[:, k, h * HALF : (h + 1) * HALF],
                     start=(n == 0),
@@ -146,23 +162,23 @@ def tile_product_of_experts_fusion_f2_kernel(
             encode(la, 1, j, h, (0, 1))
             if hook:
                 hook()
-            encode(lb, 1, j, h, (2,))
             encode(ma, 0, j, h, (0, 1))
+            encode(lb, 1, j, h, (2,))
             encode(mb, 0, j, h, (2,))
             ta = work.tile([P, HALF], F32, name="ta")
             tb = work.tile([P, HALF], F32, name="tb")
             u = work.tile([P, HALF], F32, name="u")
             v = work.tile([P, HALF], F32, name="v")
-            nc.scalar.activation(out=ta[:], in_=la[:], func=ACT.Exp, bias=v1[:, NT + j : NT + j + 1])
-            nc.scalar.activation(out=tb[:], in_=lb[:], func=ACT.Exp, bias=v1[:, 3 * NT + j : 3 * NT + j + 1])
-            nc.vector.scalar_tensor_tensor(out=u[:], in0=ma[:], scalar=v1[:, j : j + 1], in1=ta[:], op0=ALU.add, op1=ALU.mult)
-            nc.vector.scalar_tensor_tensor(out=v[:], in0=mb[:], scalar=v1[:, 2 * NT + j : 2 * NT + j + 1], in1=tb[:], op0=ALU.add, op1=ALU.mult)
+            nc.scalar.activation(out=ta[:], in_=la[:], func=ACT.Exp, bias=fa[:, NT + j : NT + j + 1])
+            nc.scalar.activation(out=tb[:], in_=lb[:], func=ACT.Exp, bias=fb[:, NT + j : NT + j + 1])
+            nc.vector.scalar_tensor_tensor(out=u[:], in0=ma[:], scalar=fa[:, j : j + 1], in1=ta[:], op0=ALU.add, op1=ALU.mult)
+            nc.vector.scalar_tensor_tensor(out=v[:], in0=mb[:], scalar=fb[:, j : j + 1], in1=tb[:], op0=ALU.add, op1=ALU.mult)
             nc.gpsimd.tensor_tensor(out=lam[:, h, j, :], in0=ta[:], in1=tb[:], op=ALU.add)
             return (h, j, u, v)
 
         def w(un, eng):
             h, j, u, v = un
-            eng.tensor_tensor(out=num[:, h, j, :], in0=u[:], in1=v[:], op=ALU.add)
+            (nc.vector if j % 2 else eng).tensor_tensor(out=num[:, h, j, :], in0=u[:], in1=v[:], op=ALU.add)
 
         def rsqrt(h, j):
             nc.scalar.activation(out=lam[:, h, j, :], in_=lam[:, h, j, :], func=ACT.Abs_reciprocal_sqrt, bias=t0[:, j : j + 1])
@@ -172,43 +188,37 @@ def tile_product_of_experts_fusion_f2_kernel(
                 out=num[:, h, j, :], in0=num[:, h, j, :], scalar=c0[:, j : j + 1], in1=lam[:, h, j, :], op0=ALU.add, op1=ALU.mult
             )
 
-        def turn_item(s, g, km, kr):
-            h, sl = divmod(s, 4)
-            bm, br = bank(km), bank(kr)
-            for b, src in ((bm, num), (br, lam)):
-                for jj in range(4):
-                    nc.tensor.transpose(b[:, P * jj : P * (jj + 1)], src[:, h, 4 * g + jj, P * sl : P * (sl + 1)], ident[:])
-            return bm, br
+        def turn_eps(h, g, u, k):
+            words = eps_sb[:].rearrange("p s n -> p (s n)").bitcast(F32)
+            b = bank(k)
+            for s in range(4):
+                first = (4 * h + s) * 512 + 256 * g + u
+                nc.tensor.transpose(b[:, P * s : P * (s + 1)], words[:, first : first + 255 : 2], ident[:])
+            return b
 
-        def z_t(s, g, bm):
-            zt = work.tile([P, 512], F32, name="zt")
-            nc.vector.tensor_tensor(out=zt[:], in0=bm[:], in1=eps_sb[:, s, 512 * g : 512 * (g + 1)], op=ALU.add)
-            return zt
+        def z_t(h, g, u, b, c):
+            js = slice(4 * g + 2 * u, 4 * g + 2 * u + 2)
+            nc.vector.tensor_tensor(
+                out=num[:, h, js, c],
+                in0=num[:, h, js, c],
+                in1=b[:].bitcast(BF16).rearrange("p (s e) -> p e s", e=2)[:, :, c],
+                op=ALU.add,
+            )
 
-        def z_z(zt, br):
-            zb = work.tile([P, 512], BF16, align_bytes=64, name="zb")
-            nc.vector.tensor_tensor(out=zb[:], in0=br[:], in1=zt[:], op=ALU.mult)
+        def z_z(h, g, c, n):
+            zb = work.tile([P, HALF * T], BF16, align_bytes=64, name="zb")
+            js = slice(4 * g, 4 * g + 4)
+            nc.vector.tensor_tensor(
+                out=zb[:, 0 : n * T].rearrange("p (c i t) -> p c t i", i=4, t=T),
+                in0=num[:, h, js, c].rearrange("p t (c i) -> p c t i", i=4),
+                in1=lam[:, h, js, c].rearrange("p t (c i) -> p c t i", i=4),
+                op=ALU.mult,
+            )
             return zb
 
-        def turn_words(s, zb, b):
-            words = zb[:].bitcast(F32)
-            for u in range(2):
-                first = 256 * u + P * (s % 2)
-                nc.tensor.transpose(b[:, first : first + P], words[:, u : u + 255 : 2], ident[:])
-
-        def z_x(b, eng):
-            zi = twice.tile([P, 256 * T], BF16, align_bytes=64, name="zi")
-            dst = zi[:].bitcast(F32).rearrange("p (c i u) -> p c u i", i=4, u=2)
-            src = b[:].rearrange("p (u c i) -> p c u i", i=4, u=2)
-            if eng == "S":
-                nc.scalar.copy(out=dst, in_=src)
-            else:
-                nc.vector.tensor_copy(out=dst, in_=src)
-            return zi
-
-        def z_q(sp, g, zi):
-            cols = slice(sp * 256, (sp + 1) * 256)
-            nc.vector.quantize_mx(out=zq[:, g, cols].bitcast(FP8X4), scales=zs[:, g, cols], in_=zi[:])
+        def z_q(h, g, c, n, zb):
+            cols = slice(h * HALF + c.start, h * HALF + c.stop)
+            nc.vector.quantize_mx(out=zq[:, g, cols].bitcast(FP8X4), scales=zs[:, g, cols], in_=zb[:, 0 : n * T])
 
         def decode_t(f, s0, ns, b):
             n = P * ns if ns == 4 else P
@@ -245,15 +255,15 @@ def tile_product_of_experts_fusion_f2_kernel(
             b = bank(k)
             decode(s, 512 * blk, b)
             yd = outs.tile([P, 512], F32, name="yd")
-            bias = cbb if blk == 2 else cab2
-            nc.vector.tensor_tensor(out=yd[:], in0=b[:], in1=bias[:], op=ALU.add)
-            dst = out_b[s * P : (s + 1) * P, :] if blk == 2 else out_a[s * P : (s + 1) * P, 512:1024]
+            bias = ball[:, 512 * blk : 512 * blk + 512]
+            nc.vector.tensor_tensor(out=yd[:], in0=b[:], in1=bias, op=ALU.add)
+            dst = out_b[s * P : (s + 1) * P, :] if blk == 2 else out_a[s * P : (s + 1) * P, 512 * blk : 512 * blk + 512]
             nc.sync.dma_start(out=dst, in_=yd[:])
 
         def acc(f, s0, ns, b):
             decode_t(f, s0, ns, b)
             yt = outs.tile([P, HALF], F32, name="yt")
-            nc.scalar.activation(out=yt[:, 0 : P * ns], in_=b[:, 0 : P * ns], func=ACT.Identity, bias=v2[:, 16 + f : 17 + f])
+            nc.scalar.activation(out=yt[:, 0 : P * ns], in_=b[:, 0 : P * ns], func=ACT.Identity, bias=v2[:, f : f + 1])
             return yt
 
         def turn(f, ns, yt, b, yo):
@@ -283,9 +293,10 @@ def tile_product_of_experts_fusion_f2_kernel(
             store(prev[0], s0, ns, prev[2], prev[0] % 4 - 1, prev[0] % 4 + 1)
 
         V, G = nc.vector, nc.gpsimd
-        it = {}
-        zi = {}
-        wb = {}
+        eb = {}
+        zb = {}
+        ALL = slice(0, 512)
+        Q = (slice(0, 256), slice(256, 512))
 
         def m4(h, g):
             for j in range(4 * g, 4 * g + 4):
@@ -295,131 +306,102 @@ def tile_product_of_experts_fusion_f2_kernel(
             for j in range(4 * g, 4 * g + 4):
                 rsqrt(h, j)
 
-        def ti(s, g, km, kr):
-            it[s, g] = list(turn_item(s, g, km, kr))
+        def ee(h, g, k0, k1):
+            eb[h, g] = (turn_eps(h, g, 0, k0), turn_eps(h, g, 1, k1))
 
-        def tz(*items):
-            for i in items:
-                it[i].append(z_t(*i, it[i][0]))
-            for i in items:
-                it[i].append(z_z(it[i][2], it[i][1]))
+        def tt(h, g, c=ALL):
+            for u in range(2):
+                z_t(h, g, u, eb[h, g][u], c)
 
-        def wd(s, g, k):
-            if s % 2 == 0:
-                wb[s // 2, g] = bank(k)
-            turn_words(s, it[s, g][3], wb[s // 2, g])
+        def zz(h, g, c=ALL):
+            zb[h, g, c.start] = z_z(h, g, c, c.stop - c.start)
 
-        def xx(sp, g, eng="S"):
-            zi[sp, g] = z_x(wb[sp, g], eng)
-
-        def qq(sp, g):
-            z_q(sp, g, zi[sp, g])
+        def qq(h, g, c=ALL):
+            z_q(h, g, c, c.stop - c.start, zb[h, g, c.start])
 
         dn = [0]
 
-        def dir_(s, blk, ks=(4, 5)):
+        def dir_(s, blk, ks):
             direct(s, blk, ks[dn[0] % len(ks)])
             dn[0] += 1
 
-        prev = None
-        for i in range(8):
-            now = unit(0, i, [4 * (i % 2) + b for b in range(4)], (lambda: turn_rows(rows1, v1, 32, bank(7))) if i == 0 else None)
-            if prev is not None:
-                w(prev, G if i % 3 else V)
-            prev = now
-            if i == 5:
-                turn_rows(rows2, v2, 28, bank(3))
-                nc.scalar.activation(out=t0[:], in_=v2[:, 0:8], func=ACT.Exp)
-                nc.vector.tensor_tensor(out=c0[:], in0=t0[:], in1=v2[:, 8:16], op=ALU.mult)
-        w(prev, G)
+        prev = [None]
+        wv = [0]
 
-        def u1(j):
-            w(unit(1, j, (0, 1, 2, 3)), G)
+        def u(h, j, ks, hook=None):
+            now = unit(h, j, ks, hook)
+            if prev[0] is not None:
+                w(prev[0], V if wv[0] % 99 == 98 else G)
+            wv[0] += 1
+            prev[0] = now
 
-        u1(0)
+        def perm(c, g, split=False):
+            perm_words(c, g, 0)
+            if split:
+                perm_scales(c, g, A)
+            perm_words(c, g, 1)
+            perm_words(c, g, 2)
+            perm_scales(c, g, B if split else slice(0, KG))
+
+        perm(1, 0, True)
+        nc.vector.tensor_copy(out=fa[:], in_=va[:].rearrange("p c t -> p (c t)"))
+        nc.vector.tensor_copy(out=fb[:], in_=vb[:].rearrange("p c t -> p (c t)"))
+        perm(0, 0, True)
+        for i in range(4):
+            u(0, i, [4 * (i % 2) + b for b in range(4)])
+            if i == 1:
+                perm(1, 1)
+            if i == 2:
+                perm(0, 1)
+        nc.scalar.activation(out=t0[:], in_=vl[:].rearrange("p c t -> p (c t)"), func=ACT.Exp)
+        nc.vector.tensor_tensor(out=c0[:], in0=t0[:], in1=vm[:].rearrange("p c t -> p (c t)"), op=ALU.mult)
+        u(0, 4, (0, 1, 2, 3))
+        ee(0, 0, 4, 5)
+        turn_rows(rows2, v2, 12, bank(6))
+        u(0, 5, (0, 1, 2, 3))
+        u(0, 6, (0, 1, 2, 3))
+        u(0, 7, (0, 1, 2, 3))
+        u(1, 0, (0, 1, 2, 3))
         r4(0, 0)
-        r4(0, 1)
         m4(0, 0)
-        ti(0, 0, 4, 5)
-        ti(1, 0, 6, 7)
-        u1(1)
+        tt(0, 0)
+        zz(0, 0)
+        ee(0, 1, 4, 5)
+        r4(0, 1)
         m4(0, 1)
-        tz((0, 0), (1, 0))
-        ti(0, 1, 4, 5)
-        u1(2)
-        wd(0, 0, 6)
-        wd(1, 0, 6)
-        xx(0, 0)
-        tz((0, 1))
-        u1(3)
-        ti(1, 1, 4, 5)
-        tz((1, 1))
-        wd(0, 1, 7)
-        wd(1, 1, 7)
-        xx(0, 1)
-        u1(4)
-        ti(2, 0, 4, 5)
+        u(1, 1, (0, 1, 2, 3))
         qq(0, 0)
-        tz((2, 0))
+        u(1, 2, (0, 1, 2, 3))
+        tt(0, 1)
+        u(1, 3, (0, 1, 2, 3))
+        zz(0, 1)
+        ee(1, 0, 4, 5)
+        u(1, 4, (0, 1, 2, 3))
         qq(0, 1)
-        u1(5)
-        ti(3, 0, 4, 5)
-        tz((3, 0))
-        wd(2, 0, 6)
-        wd(3, 0, 6)
-        xx(1, 0)
-        u1(6)
-        ti(2, 1, 4, 5)
-        tz((2, 1))
-        qq(1, 0)
-        u1(7)
-        ti(3, 1, 4, 5)
-        tz((3, 1))
-        wd(2, 1, 7)
-        wd(3, 1, 7)
-        xx(1, 1)
+        u(1, 5, (0, 1, 2, 3))
+        u(1, 6, (0, 1, 2, 3))
+        u(1, 7, (0, 1, 2, 3))
+        w(prev[0], G)
         r4(1, 0)
-        r4(1, 1)
-        dir_(0, 2, (0, 1))
-        dir_(0, 1, (0, 1))
-        dir_(1, 2, (0, 1))
-        dir_(1, 1, (0, 1))
         m4(1, 0)
-        ti(4, 0, 4, 5)
-        ti(5, 0, 6, 7)
-        qq(1, 1)
+        tt(1, 0)
+        zz(1, 0, Q[0])
+        zz(1, 0, Q[1])
+        ee(1, 1, 4, 5)
+        r4(1, 1)
+        qq(1, 0, Q[0])
+        qq(1, 0, Q[1])
+        run(0, 4, [8, 9], (6,), (7,))
         m4(1, 1)
-        tz((4, 0), (5, 0))
-        ti(4, 1, 4, 5)
-        ti(5, 1, 6, 7)
-        run(0, 4, [0, 1], (2,), (3,))
-        wd(4, 0, 0)
-        wd(5, 0, 0)
-        xx(2, 0)
-        tz((4, 1), (5, 1))
-        wd(4, 1, 1)
-        wd(5, 1, 1)
-        xx(2, 1)
-        ti(6, 0, 4, 5)
-        ti(7, 0, 6, 7)
-        run(0, 4, [2, 3], (2,), (3,))
-        dir_(2, 2, (2, 3))
-        qq(2, 0)
-        tz((6, 0), (7, 0))
-        dir_(2, 1, (2, 3))
-        qq(2, 1)
-        ti(6, 1, 4, 5)
-        ti(7, 1, 6, 7)
-        wd(6, 0, 0)
-        wd(7, 0, 0)
-        xx(3, 0)
-        tz((6, 1), (7, 1))
-        wd(6, 1, 1)
-        wd(7, 1, 1)
-        xx(3, 1)
-        dir_(3, 2, (2, 3))
-        qq(3, 0)
-        dir_(3, 1, (2, 3))
-        qq(3, 1)
-        run(4, 2, [0, 1, 2, 3], (4, 5), (6, 7), lambda n: dir_(4 + n // 2, 1 + n % 2, (2, 3)))
-        run(6, 2, [0, 1, 2, 3], (4, 5), (6, 7), lambda n: dir_(6 + n // 2, 1 + n % 2, (0, 1)))
+        tt(1, 1, Q[0])
+        zz(1, 1, Q[0])
+        run(0, 4, [10, 11, 0, 1], (6, 0), (7, 1))
+        qq(1, 1, Q[0])
+        tt(1, 1, Q[1])
+        zz(1, 1, Q[1])
+        run(0, 4, [2, 3], (6, 0), (7, 1))
+        for s in range(4):
+            dir_(s, 1, (2, 3))
+        qq(1, 1, Q[1])
+        run(4, 2, [0, 1, 2, 3], (6, 4), (7, 5), lambda n: dir_(4 + n // 2, 1 + n % 2, (0, 1)))
+        run(6, 2, [0, 1, 2, 3], (6, 4), (7, 5), lambda n: dir_(6 + n // 2, 1 + n % 2, (2, 3)))

from contextlib import ExitStack

import concourse.mybir as mybir
from concourse.masks import make_identity

F32 = mybir.dt.float32
BF16 = mybir.dt.bfloat16
U8 = mybir.dt.uint8
U32 = mybir.dt.uint32
I32 = mybir.dt.int32
FP4X4 = mybir.dt.float4_e2m1fn_x4
FP8X4 = mybir.dt.float8_e4m3fn_x4
ACT = mybir.ActivationFunctionType
ALU = mybir.AluOpType

P = 128
M, KA, KB, N = 1024, 1024, 512, 1024
FLOPS = 2 * M * (2 * N * (KA + KB) + N * (KA + KB))

HALF = 512
GA = 2
KG = 3
T = 4
NT = N // P
E = 2


def tile_product_of_experts_fusion_f2_kernel(
    tc, xa_words, xa_scales, xb_words, xb_scales, wa_words, wa_scales, wb_words, wb_scales,
    ba, bb, prior_mean, prior_logprec, eps, da_words, da_scales, db_words, db_scales, ca, cb, out_a, out_b,
):
    nc = tc.nc
    with ExitStack() as ctx:
        keep = ctx.enter_context(tc.tile_pool(name="keep", bufs=1))
        work = ctx.enter_context(tc.tile_pool(name="work", bufs=4))
        twice = ctx.enter_context(tc.tile_pool(name="twice", bufs=2))
        outs = ctx.enter_context(tc.tile_pool(name="outs", bufs=3))
        psum = ctx.enter_context(tc.psum_pool(name="psum", bufs=1))
        ctx.enter_context(tc.manual_schedule(engines={mybir.EngineType.Activation, mybir.EngineType.SP}))

        def bank(i, dt=F32):
            return psum.tile([P, 2048 // (4 if dt == F32 else 2)], dt, tag="b%d" % i, name="b%d" % i)

        xw = keep.tile([P, KG, 2 * M], U8, align_bytes=64, name="xw")
        xs = keep.tile([P, KG, M], U8, align_bytes=64, name="xs")
        ww = keep.tile([P, KG, 4 * N], U8, align_bytes=64, name="ww")
        ws = keep.tile([P, KG, 2 * N], U8, align_bytes=64, name="ws")
        wp = keep.tile([P, 2, E, KG, 1024], U8, align_bytes=64, name="wp")
        wsp = keep.tile([P, 2, E, KG, 512], U8, align_bytes=64, name="wsp")
        dw = keep.tile([P, E, 3072], U8, align_bytes=64, name="dw")
        dsc = keep.tile([P, E, 1536], U8, align_bytes=64, name="dsc")
        eps_sb = keep.tile([P, 8, N], BF16, align_bytes=64, name="eps_sb")
        lam = keep.tile([P, 2, NT, HALF], F32, align_bytes=64, name="lam")
        num = keep.tile([P, 2, NT, HALF], F32, align_bytes=64, name="num")
        zq = keep.tile([P, E, M], U32, align_bytes=64, name="zq")
        zs = keep.tile([P, E, M], U8, align_bytes=64, name="zs")
        ident = keep.tile([P, P], F32, align_bytes=64, name="ident")
        warm = keep.tile([P, 1], F32, name="warm")
        warm2 = keep.tile([P, 1], F32, name="warm2")
        rows2 = keep.tile([P, P], BF16, name="rows2")
        v2 = keep.tile([P, 12], F32, name="v2")
        t0 = keep.tile([P, NT], F32, name="t0")
        c0 = keep.tile([P, NT], F32, name="c0")
        ball = keep.tile([P, KA + KB], BF16, name="ball")

        for k in (slice(0, GA), slice(GA, KG)):
            nc.vector.memset(xs[:, k, :].rearrange("p a n -> p (a n)").bitcast(I32), 0)
            nc.vector.memset(ws[:, k, :].rearrange("p a n -> p (a n)").bitcast(I32), 0)
        nc.vector.memset(warm[:], 0.0)
        va = keep.tile([P, 4, T], BF16, name="va")
        vb = keep.tile([P, 4, T], BF16, name="vb")
        vm = keep.tile([P, E, T], BF16, name="vm")
        vl = keep.tile([P, E, T], BF16, name="vl")
        fa = keep.tile([P, 4 * T], F32, name="fa")
        fb = keep.tile([P, 4 * T], F32, name="fb")
        nc.gpsimd.dma_start(out=va[:], in_=ba.rearrange("(c p t) -> p c t", p=P, t=T))
        nc.gpsimd.dma_start(out=vb[:], in_=bb.rearrange("(c p t) -> p c t", p=P, t=T))
        make_identity(nc, ident[:])

        def load_scales(engs, plane, groups, cols, src):
            for r in range(4):
                engs[r].dma_start(
                    out=plane[r:P:32, groups, cols].bitcast(I32),
                    in_=src[:, r:16:4, :].bitcast(I32).rearrange("g q n -> q g n"),
                )

        def load_words(dst, src):
            nc.sync.dma_start(out=dst.bitcast(I32), in_=src.bitcast(I32).rearrange("g p n -> p g n"))

        A = slice(0, GA)
        B = slice(GA, KG)

        def wcols(c, g):
            return slice((c * N + g * 512) * 2, (c * N + (g + 1) * 512) * 2)

        def xcols(h):
            return slice(h * 2 * HALF, (h + 1) * 2 * HALF)

        load_words(ww[:, A, wcols(1, 0)], wa_words[:, :, wcols(1, 0)])
        load_words(xw[:, A, xcols(0)], xa_words[:, :, xcols(0)])
        load_scales([nc.sync] * 4, xs, A, slice(0, M), xa_scales)
        load_scales([nc.scalar] * 4, ws, A, slice(0, 2 * N), wa_scales)
        nc.scalar.activation(out=warm2[:], in_=warm[:], func=ACT.Exp)
        load_words(ww[:, B, wcols(1, 0)], wb_words[:, :, wcols(1, 0)])
        load_words(xw[:, B, xcols(0)], xb_words[:, :, xcols(0)])
        load_scales([nc.sync] * 4, xs, B, slice(0, M), xb_scales)
        load_scales([nc.sync] * 4, ws, B, slice(0, 2 * N), wb_scales)
        nc.gpsimd.memset(dsc[:].rearrange("p a n -> p (a n)").bitcast(I32), 0)
        nc.gpsimd.memset(rows2[:], 0.0)
        nc.gpsimd.dma_start(out=vl[:], in_=prior_logprec.rearrange("(c p t) -> p c t", p=P, t=T))
        nc.gpsimd.dma_start(out=vm[:], in_=prior_mean.rearrange("(c p t) -> p c t", p=P, t=T))
        nc.gpsimd.dma_start(out=rows2[0:8, :], in_=ca.rearrange("(c p) -> c p", p=P))
        nc.gpsimd.dma_start(out=rows2[8:12, :], in_=cb.rearrange("(c p) -> c p", p=P))
        for c, g in ((0, 0), (1, 1), (0, 1)):
            load_words(ww[:, A, wcols(c, g)], wa_words[:, :, wcols(c, g)])
            load_words(ww[:, B, wcols(c, g)], wb_words[:, :, wcols(c, g)])
        load_words(xw[:, A, xcols(1)], xa_words[:, :, xcols(1)])
        load_words(xw[:, B, xcols(1)], xb_words[:, :, xcols(1)])
        eps_r = eps.rearrange("(s p) n -> p s n", p=P)
        nc.sync.dma_start(out=eps_sb[:, 0:4, :], in_=eps_r[:, 0:4, :])
        nc.sync.dma_start(out=eps_sb[:, 4:8, :], in_=eps_r[:, 4:8, :])
        load_words(dw[:, :, 0:2048], da_words)
        load_words(dw[:, :, 2048:3072], db_words)
        load_scales([nc.sync] * 4, dsc, slice(0, E), slice(0, 1024), da_scales)
        load_scales([nc.sync] * 4, dsc, slice(0, E), slice(1024, 1536), db_scales)
        nc.sync.dma_start(out=ball[:, 0:KA], in_=ca.partition_broadcast(P))
        nc.sync.dma_start(out=ball[:, KA : KA + KB], in_=cb.partition_broadcast(P))

        def perm_words(c, g, k):
            nc.vector.tensor_copy(
                out=wp[:, c, g, k, :].rearrange("p (t m b) -> p t m b", t=T, b=2),
                in_=ww[:, k, wcols(c, g)].rearrange("p (m t b) -> p t m b", t=T, b=2),
            )

        def perm_scales(c, g, ks):
            nc.vector.tensor_copy(
                out=wsp[:, c, g, ks, :].rearrange("p k (t m) -> p k t m", t=T),
                in_=ws[:, ks, c * N + g * 512 : c * N + (g + 1) * 512].rearrange("p k (m t) -> p k t m", t=T),
            )

        def turn_rows(rows, vecs, n, b):
            full = work.tile([P, P], F32, name="full")
            nc.vector.tensor_copy(out=full[:], in_=rows[:])
            nc.tensor.transpose(b[:, 0:P], full[:], ident[:])
            nc.vector.tensor_copy(out=vecs[:], in_=b[:, 0:n])

        def encode(dst, c, j, h, ks):
            for n, k in enumerate(ks):
                g, t = divmod(j, T)
                nc.tensor.matmul_mx(
                    out=dst[:],
                    lhsT=wp[:, c, g, k, 256 * t : 256 * (t + 1)].bitcast(FP4X4),
                    lhsT_scale=wsp[:, c, g, k, P * t : P * (t + 1)],
                    rhs=xw[:, k, xcols(h)].bitcast(FP4X4),
                    rhs_scale=xs[:, k, h * HALF : (h + 1) * HALF],
                    start=(n == 0),
                    stop=(n == len(ks) - 1),
                )

        def unit(h, j, ks, hook=None):
            la, lb, ma, mb = [bank(k) for k in ks]
            encode(la, 1, j, h, (0, 1))
            if hook:
                hook()
            encode(ma, 0, j, h, (0, 1))
            encode(lb, 1, j, h, (2,))
            encode(mb, 0, j, h, (2,))
            ta = work.tile([P, HALF], F32, name="ta")
            tb = work.tile([P, HALF], F32, name="tb")
            u = work.tile([P, HALF], F32, name="u")
            v = work.tile([P, HALF], F32, name="v")
            nc.scalar.activation(out=ta[:], in_=la[:], func=ACT.Exp, bias=fa[:, NT + j : NT + j + 1])
            nc.scalar.activation(out=tb[:], in_=lb[:], func=ACT.Exp, bias=fb[:, NT + j : NT + j + 1])
            nc.vector.scalar_tensor_tensor(out=u[:], in0=ma[:], scalar=fa[:, j : j + 1], in1=ta[:], op0=ALU.add, op1=ALU.mult)
            nc.vector.scalar_tensor_tensor(out=v[:], in0=mb[:], scalar=fb[:, j : j + 1], in1=tb[:], op0=ALU.add, op1=ALU.mult)
            nc.gpsimd.tensor_tensor(out=lam[:, h, j, :], in0=ta[:], in1=tb[:], op=ALU.add)
            return (h, j, u, v)

        def w(un, eng):
            h, j, u, v = un
            (nc.vector if j % 2 else eng).tensor_tensor(out=num[:, h, j, :], in0=u[:], in1=v[:], op=ALU.add)

        def rsqrt(h, j):
            nc.scalar.activation(out=lam[:, h, j, :], in_=lam[:, h, j, :], func=ACT.Abs_reciprocal_sqrt, bias=t0[:, j : j + 1])

        def z_m(h, j):
            nc.vector.scalar_tensor_tensor(
                out=num[:, h, j, :], in0=num[:, h, j, :], scalar=c0[:, j : j + 1], in1=lam[:, h, j, :], op0=ALU.add, op1=ALU.mult
            )

        def turn_eps(h, g, u, k):
            words = eps_sb[:].rearrange("p s n -> p (s n)").bitcast(F32)
            b = bank(k)
            for s in range(4):
                first = (4 * h + s) * 512 + 256 * g + u
                nc.tensor.transpose(b[:, P * s : P * (s + 1)], words[:, first : first + 255 : 2], ident[:])
            return b

        def z_t(h, g, u, b, c):
            js = slice(4 * g + 2 * u, 4 * g + 2 * u + 2)
            nc.vector.tensor_tensor(
                out=num[:, h, js, c],
                in0=num[:, h, js, c],
                in1=b[:].bitcast(BF16).rearrange("p (s e) -> p e s", e=2)[:, :, c],
                op=ALU.add,
            )

        def z_z(h, g, c, n):
            zb = work.tile([P, HALF * T], BF16, align_bytes=64, name="zb")
            js = slice(4 * g, 4 * g + 4)
            nc.vector.tensor_tensor(
                out=zb[:, 0 : n * T].rearrange("p (c i t) -> p c t i", i=4, t=T),
                in0=num[:, h, js, c].rearrange("p t (c i) -> p c t i", i=4),
                in1=lam[:, h, js, c].rearrange("p t (c i) -> p c t i", i=4),
                op=ALU.mult,
            )
            return zb

        def z_q(h, g, c, n, zb):
            cols = slice(h * HALF + c.start, h * HALF + c.stop)
            nc.vector.quantize_mx(out=zq[:, g, cols].bitcast(FP8X4), scales=zs[:, g, cols], in_=zb[:, 0 : n * T])

        def decode_t(f, s0, ns, b):
            n = P * ns if ns == 4 else P
            for c in range(P * ns // n):
                cols = slice(s0 * P + c * n, s0 * P + (c + 1) * n)
                for e in range(E):
                    nc.tensor.matmul_mx(
                        out=b[:, c * n : (c + 1) * n],
                        lhsT=dw[:, e, 256 * f : 256 * (f + 1)].bitcast(FP4X4),
                        lhsT_scale=dsc[:, e, P * f : P * (f + 1)],
                        rhs=zq[:, e, cols].bitcast(FP8X4),
                        rhs_scale=zs[:, e, cols],
                        start=(e == 0),
                        stop=(e == E - 1),
                    )

        def decode(s, first, b):
            cols = slice(s * P, (s + 1) * P)
            for e in range(E):
                nc.tensor.matmul_mx(
                    out=b[:],
                    lhsT=zq[:, e, cols].bitcast(FP8X4),
                    lhsT_scale=zs[:, e, cols],
                    rhs=dw[:, e, 2 * first : 2 * (first + 512)].bitcast(FP4X4),
                    rhs_scale=dsc[:, e, first : first + 512],
                    start=(e == 0),
                    stop=(e == E - 1),
                )

        out_ar = out_a.rearrange("(s p) n -> p s n", p=P)
        out_br = out_b.rearrange("(s p) n -> p s n", p=P)

        def direct(s, blk, k):
            b = bank(k)
            decode(s, 512 * blk, b)
            yd = outs.tile([P, 512], F32, name="yd")
            bias = ball[:, 512 * blk : 512 * blk + 512]
            nc.vector.tensor_tensor(out=yd[:], in0=b[:], in1=bias, op=ALU.add)
            dst = out_b[s * P : (s + 1) * P, :] if blk == 2 else out_a[s * P : (s + 1) * P, 512 * blk : 512 * blk + 512]
            nc.sync.dma_start(out=dst, in_=yd[:])

        def acc(f, s0, ns, b):
            decode_t(f, s0, ns, b)
            yt = outs.tile([P, HALF], F32, name="yt")
            nc.scalar.activation(out=yt[:, 0 : P * ns], in_=b[:, 0 : P * ns], func=ACT.Identity, bias=v2[:, f : f + 1])
            return yt

        def turn(f, ns, yt, b, yo):
            for s in range(ns):
                nc.tensor.transpose(b[:, P * s : P * (s + 1)], yt[:, P * s : P * (s + 1)], ident[:])
            q = f % 4
            nc.scalar.copy(out=yo[:, 0:ns, P * q : P * (q + 1)], in_=b[:, 0 : P * ns].rearrange("p (s n) -> p s n", s=ns))

        def store(f, s0, ns, yo, q0, q1):
            dst = (out_br if f >= 8 else out_ar)[:, s0 : s0 + ns, (f // 4 % 2) * 512 + P * q0 : (f // 4 % 2) * 512 + P * q1]
            nc.sync.dma_start(out=dst, in_=yo[:, 0:ns, P * q0 : P * q1])

        def run(s0, ns, fs, accs, turns, hook=lambda n: None):
            prev = None
            yo = None
            for n, f in enumerate(fs):
                if n == 0 or f % 4 == 0:
                    nxt = outs.tile([P, 4, 512], F32, name="yo")
                yt = acc(f, s0, ns, bank(accs[n % len(accs)]))
                if prev is not None:
                    turn(prev[0], ns, prev[1], bank(turns[(n - 1) % len(turns)]), prev[2])
                    if prev[0] % 2 == 1:
                        store(prev[0], s0, ns, prev[2], prev[0] % 4 - 1, prev[0] % 4 + 1)
                prev = (f, yt, nxt)
                hook(n)
            turn(prev[0], ns, prev[1], bank(turns[(len(fs) - 1) % len(turns)]), prev[2])
            store(prev[0], s0, ns, prev[2], prev[0] % 4 - 1, prev[0] % 4 + 1)

        V, G = nc.vector, nc.gpsimd
        eb = {}
        zb = {}
        ALL = slice(0, 512)
        Q = (slice(0, 256), slice(256, 512))

        def m4(h, g):
            for j in range(4 * g, 4 * g + 4):
                z_m(h, j)

        def r4(h, g):
            for j in range(4 * g, 4 * g + 4):
                rsqrt(h, j)

        def ee(h, g, k0, k1):
            eb[h, g] = (turn_eps(h, g, 0, k0), turn_eps(h, g, 1, k1))

        def tt(h, g, c=ALL):
            for u in range(2):
                z_t(h, g, u, eb[h, g][u], c)

        def zz(h, g, c=ALL):
            zb[h, g, c.start] = z_z(h, g, c, c.stop - c.start)

        def qq(h, g, c=ALL):
            z_q(h, g, c, c.stop - c.start, zb[h, g, c.start])

        dn = [0]

        def dir_(s, blk, ks):
            direct(s, blk, ks[dn[0] % len(ks)])
            dn[0] += 1

        prev = [None]
        wv = [0]

        def u(h, j, ks, hook=None):
            now = unit(h, j, ks, hook)
            if prev[0] is not None:
                w(prev[0], V if wv[0] % 99 == 98 else G)
            wv[0] += 1
            prev[0] = now

        def perm(c, g, split=False):
            perm_words(c, g, 0)
            if split:
                perm_scales(c, g, A)
            perm_words(c, g, 1)
            perm_words(c, g, 2)
            perm_scales(c, g, B if split else slice(0, KG))

        perm(1, 0, True)
        nc.vector.tensor_copy(out=fa[:], in_=va[:].rearrange("p c t -> p (c t)"))
        nc.vector.tensor_copy(out=fb[:], in_=vb[:].rearrange("p c t -> p (c t)"))
        perm(0, 0, True)
        for i in range(4):
            u(0, i, [4 * (i % 2) + b for b in range(4)])
            if i == 1:
                perm(1, 1)
            if i == 2:
                perm(0, 1)
        nc.scalar.activation(out=t0[:], in_=vl[:].rearrange("p c t -> p (c t)"), func=ACT.Exp)
        nc.vector.tensor_tensor(out=c0[:], in0=t0[:], in1=vm[:].rearrange("p c t -> p (c t)"), op=ALU.mult)
        u(0, 4, (0, 1, 2, 3))
        ee(0, 0, 4, 5)
        turn_rows(rows2, v2, 12, bank(6))
        u(0, 5, (0, 1, 2, 3))
        u(0, 6, (0, 1, 2, 3))
        u(0, 7, (0, 1, 2, 3))
        u(1, 0, (0, 1, 2, 3))
        r4(0, 0)
        m4(0, 0)
        tt(0, 0)
        zz(0, 0)
        ee(0, 1, 4, 5)
        r4(0, 1)
        m4(0, 1)
        u(1, 1, (0, 1, 2, 3))
        qq(0, 0)
        u(1, 2, (0, 1, 2, 3))
        tt(0, 1)
        u(1, 3, (0, 1, 2, 3))
        zz(0, 1)
        ee(1, 0, 4, 5)
        u(1, 4, (0, 1, 2, 3))
        qq(0, 1)
        u(1, 5, (0, 1, 2, 3))
        u(1, 6, (0, 1, 2, 3))
        u(1, 7, (0, 1, 2, 3))
        w(prev[0], G)
        r4(1, 0)
        m4(1, 0)
        tt(1, 0)
        zz(1, 0, Q[0])
        zz(1, 0, Q[1])
        ee(1, 1, 4, 5)
        r4(1, 1)
        qq(1, 0, Q[0])
        qq(1, 0, Q[1])
        run(0, 4, [8, 9], (6,), (7,))
        m4(1, 1)
        tt(1, 1, Q[0])
        zz(1, 1, Q[0])
        run(0, 4, [10, 11, 0, 1], (6, 0), (7, 1))
        qq(1, 1, Q[0])
        tt(1, 1, Q[1])
        zz(1, 1, Q[1])
        run(0, 4, [2, 3], (6, 0), (7, 1))
        for s in range(4):
            dir_(s, 1, (2, 3))
        qq(1, 1, Q[1])
        run(4, 2, [0, 1, 2, 3], (6, 4), (7, 5), lambda n: dir_(4 + n // 2, 1 + n % 2, (0, 1)))
        run(6, 2, [0, 1, 2, 3], (6, 4), (7, 5), lambda n: dir_(6 + n // 2, 1 + n % 2, (2, 3)))
